import numpy as np
import ml_dtypes


def mxq(x, axis, fmt="e4m3"):
    dtype, down = {"e4m3": (ml_dtypes.float8_e4m3fn, 7), "e5m2": (ml_dtypes.float8_e5m2, 14)}[fmt]
    v = np.moveaxis(np.asarray(x, np.float32).astype(ml_dtypes.bfloat16).astype(np.float64), axis, -1)
    blocks = v.reshape(v.shape[:-1] + (-1, 32))
    amax = np.abs(blocks).max(-1, keepdims=True)
    byte = np.maximum(np.where(amax > 0, np.frexp(amax)[1] - 1 + 127, 0) - down, 1)
    scale = np.exp2(byte - 127.0)
    codes = (blocks / scale).astype(np.float32).astype(dtype).astype(np.float64)
    return np.moveaxis((codes * scale).reshape(v.shape), -1, axis)


WIDE = False


def mx_kscale(k):
    if not WIDE:
        return np.ones(k)
    levels = np.array([30, -30])
    if k % 512:
        return np.exp2(np.random.permutation(np.resize(levels, k // 32))).repeat(32)
    a = np.empty((k // 512, 16))
    for p in range(k // 512):
        a[p, :8] = np.random.permutation(np.resize(levels, 8))
        for g in range(8):
            far = levels[np.abs(levels - a[p, g]) >= 10]
            a[p, g + 8] = far[np.random.randint(len(far))]
    return np.exp2(a.ravel()).repeat(32)


def f64(x):
    return np.asarray(x).astype(np.float64)


E2M1 = np.array([0.0, 0.5, 1.0, 1.5, 2.0, 3.0, 4.0, 6.0, -0.0, -0.5, -1.0, -1.5, -2.0, -3.0, -4.0, -6.0])


def pack_weight(w, fmt):
    k, n = w.shape
    w = f64(np.asarray(w, np.float32).astype(ml_dtypes.bfloat16)).reshape(k // 32, 32, n)
    amax = np.abs(w).max(1)
    if fmt == "e4m3":
        byte = np.frexp(amax)[1] - 1 + 127 - 7
    else:
        mant, ex = np.frexp(amax / 6.0)
        byte = np.where(mant > 0.5, ex, ex - 1) + 127
    byte = np.clip(np.where(amax > 0, byte, 1), 1, 254)
    scaled = (w * np.exp2(127.0 - byte)[:, None, :]).reshape(k, n).astype(np.float32)
    by_word = np.ascontiguousarray(scaled.reshape(k // 512, 128, 4, n).transpose(0, 1, 3, 2))
    if fmt == "e4m3":
        words = by_word.astype(ml_dtypes.float8_e4m3fn).view(np.uint8)
    else:
        c = by_word.astype(ml_dtypes.float4_e2m1fn).view(np.uint8) & 0xF
        words = (c[..., 0::2] | (c[..., 1::2] << 4)).reshape(k // 512, 128, 2 * n)
    return np.ascontiguousarray(words), np.ascontiguousarray(byte.astype(np.uint8).reshape(k // 512, 16, n))


def unpack_weight(words, scales, fmt):
    g, _, n = scales.shape
    words = np.ascontiguousarray(words).reshape(g, 128, n, -1)
    if fmt == "e4m3":
        vals = words.view(ml_dtypes.float8_e4m3fn).astype(np.float64)
    else:
        nib = np.empty((g, 128, n, 4), np.uint8)
        nib[..., 0::2] = words & 0xF
        nib[..., 1::2] = words >> 4
        vals = E2M1[nib]
    vals = vals * np.repeat(np.exp2(scales.astype(np.float64) - 127.0), 8, axis=1)[..., None]
    return vals.transpose(0, 1, 3, 2).reshape(g * 512, n)


O, K, M, T = 1024, 2560, 512, 512


def setup_inputs():
    n = np.random.standard_normal
    s = mx_kscale(K)[:, None]
    dy = np.exp(0.5 * n((1, T))) * n((K, T))
    w = n((K, M)) / np.sqrt(K) / s
    p_w8 = pack_weight(w[:O], "e4m3")
    p_w4 = pack_weight(w[O:], "e2m1")
    return {
        "dy": (dy * s).astype(np.float32),
        "w8_words": p_w8[0],
        "w8_scales": p_w8[1],
        "w4_words": p_w4[0],
        "w4_scales": p_w4[1],
    }


def reference(dy, w8_words, w8_scales, w4_words, w4_scales):
    dy_ = mxq(f64(dy), 0, "e5m2")
    w8_ = unpack_weight(w8_words, w8_scales, "e4m3")
    w4_ = unpack_weight(w4_words, w4_scales, "e2m1")
    y = dy_[:O].T @ w8_ + dy_[O:].T @ w4_
    return y

@@ -1,0 +1,140 @@
+from contextlib import ExitStack
+
+import concourse.mybir as mybir
+
+K, T, D = 2560, 512, 512
+FLOPS = 2 * K * T * D
+
+F32 = mybir.dt.float32
+BF16 = mybir.dt.bfloat16
+I32 = mybir.dt.int32
+U32 = mybir.dt.uint32
+U8 = mybir.dt.uint8
+E5M2X4 = mybir.dt.float8_e5m2_x4
+E4M3X4 = mybir.dt.float8_e4m3fn_x4
+E2M1X4 = mybir.dt.float4_e2m1fn_x4
+
+P = 128
+J = 4
+PASSES = 5
+W8_PASSES = 2
+W4_PASSES = 3
+BLOCKS = 4
+HALF = T // 2
+V_COLS = 320
+
+
+def load_scales(nc, plane, scales, passes):
+    rows = scales.bitcast(I32).rearrange("a (q r) d -> r q a d", r=4)
+    for r in range(4):
+        nc.gpsimd.dma_start(
+            out=plane[r:P:32, :].bitcast(I32).rearrange("q (a d) -> q a d", a=passes), in_=rows[r]
+        )
+
+
+def interleave(copy, grouped, raw, t0, t1):
+    copy(
+        out=grouped[:, t0:t1, :].rearrange("p (c i) j -> p c j i", i=4),
+        in_=raw[:, :, t0:t1].rearrange("p j (c i) -> p c j i", i=4),
+    )
+
+
+def tile_mix_dyq_tm_none_kernel(tc, dy, w8_words, w8_scales, w4_words, w4_scales, out):
+    nc = tc.nc
+    dy_rows = dy.rearrange("(g p j) t -> g p j t", p=P, j=J)
+
+    with ExitStack() as ctx:
+        keep = ctx.enter_context(tc.tile_pool(name="keep", bufs=1))
+        psum = ctx.enter_context(tc.psum_pool(name="psum", bufs=1))
+        ctx.enter_context(tc.manual_schedule())
+
+        raw = [keep.tile([P, J, T], F32, name="raw%d" % g, align_bytes=64) for g in range(PASSES - 1)]
+        grouped = [keep.tile([P, T, J], BF16, name="grouped%d" % g, align_bytes=64) for g in range(PASSES - 1)]
+        codes = [keep.tile([P, T], U32, name="codes%d" % g, align_bytes=64) for g in range(PASSES - 1)]
+        scales = [keep.tile([P, T], U8, name="scales%d" % g, align_bytes=64) for g in range(PASSES - 1)]
+        last_raw = [keep.tile([P, J, P], F32, name="last_raw%d" % b, align_bytes=64) for b in range(BLOCKS)]
+        last_grouped = [keep.tile([P, P, J], BF16, name="last_grouped%d" % b, align_bytes=64) for b in range(BLOCKS)]
+        last_codes = [keep.tile([P, P], U32, name="last_codes%d" % b, align_bytes=64) for b in range(BLOCKS)]
+        last_scales = [keep.tile([P, P], U8, name="last_scales%d" % b, align_bytes=64) for b in range(BLOCKS)]
+        w8 = keep.tile([P, W8_PASSES, D * 4], U8, name="w8", align_bytes=64)
+        w4 = keep.tile([P, W4_PASSES, D * 2], U8, name="w4", align_bytes=64)
+        w8_plane = keep.tile([P, W8_PASSES * D], U8, name="w8_plane", align_bytes=64)
+        w4_plane = keep.tile([P, W4_PASSES * D], U8, name="w4_plane", align_bytes=64)
+        result = [keep.tile([P, D], F32, name="result%d" % b, align_bytes=64) for b in range(BLOCKS)]
+        table_in = keep.tile([P, 1], F32, name="table_in")
+        table_out = keep.tile([P, 1], F32, name="table_out")
+        acc = [psum.tile([P, D], F32, name="acc%d" % b) for b in range(BLOCKS)]
+
+        nc.sync.dma_start(out=raw[0][:], in_=dy_rows[0])
+        nc.sync.dma_start(
+            out=w8[:].rearrange("p a b -> p (a b)").bitcast(I32).rearrange("p (a b) -> p a b", a=W8_PASSES),
+            in_=w8_words.rearrange("a p d i -> p a (d i)").bitcast(I32),
+        )
+        nc.sync.dma_start(out=raw[1][:], in_=dy_rows[1])
+        nc.sync.dma_start(
+            out=w4[:].rearrange("p a b -> p (a b)").bitcast(I32).rearrange("p (a b) -> p a b", a=W4_PASSES),
+            in_=w4_words.rearrange("a p b -> p a b").bitcast(I32),
+        )
+        nc.sync.dma_start(out=raw[2][:], in_=dy_rows[2])
+        nc.sync.dma_start(out=raw[3][:], in_=dy_rows[3])
+        for b in range(BLOCKS):
+            nc.sync.dma_start(out=last_raw[b][:], in_=dy_rows[PASSES - 1][:, :, b * P : (b + 1) * P])
+
+        nc.vector.memset(w8_plane[:].bitcast(I32), 0)
+        nc.vector.memset(w4_plane[:].bitcast(I32), 0)
+        nc.vector.memset(table_in[:], 0.0)
+        load_scales(nc, w8_plane, w8_scales, W8_PASSES)
+        load_scales(nc, w4_plane, w4_scales, W4_PASSES)
+
+        nc.scalar.copy(out=table_out[:], in_=table_in[:])
+
+        def multiply(g, b, b_codes, b_scales):
+            if g < W8_PASSES:
+                words = w8[:, g, :].bitcast(E4M3X4)
+                plane = w8_plane[:, g * D : (g + 1) * D]
+            else:
+                a = g - W8_PASSES
+                words = w4[:, a, :].bitcast(E2M1X4)
+                plane = w4_plane[:, a * D : (a + 1) * D]
+            nc.tensor.matmul_mx(
+                out=acc[b][:],
+                lhsT=b_codes.bitcast(E5M2X4),
+                lhsT_scale=b_scales,
+                rhs=words,
+                rhs_scale=plane,
+                start=(g == 0),
+                stop=(g == PASSES - 1),
+            )
+
+        for g in range(PASSES - 1):
+            interleave(nc.scalar.copy, grouped[g], raw[g], V_COLS, T)
+            interleave(nc.vector.tensor_copy, grouped[g], raw[g], 0, HALF)
+            interleave(nc.vector.tensor_copy, grouped[g], raw[g], HALF, V_COLS)
+            for t0 in (0, HALF):
+                nc.vector.quantize_mx(
+                    out=codes[g][:, t0 : t0 + HALF].bitcast(E5M2X4),
+                    scales=scales[g][:, t0 : t0 + HALF],
+                    in_=grouped[g][:, t0 : t0 + HALF, :].rearrange("p t j -> p (t j)"),
+                )
+            for b in range(BLOCKS):
+                cols = slice(b * P, (b + 1) * P)
+                multiply(g, b, codes[g][:, cols], scales[g][:, cols])
+
+        def finish(copy, b, d0, d1):
+            copy(out=result[b][:, d0:d1], in_=acc[b][:, d0:d1])
+            nc.sync.dma_start(out=out[b * P : (b + 1) * P, d0:d1], in_=result[b][:, d0:d1])
+
+        for b in range(BLOCKS + 1):
+            if b < BLOCKS:
+                interleave(nc.vector.tensor_copy, last_grouped[b], last_raw[b], 0, P)
+            if b > 0:
+                nc.vector.quantize_mx(
+                    out=last_codes[b - 1][:].bitcast(E5M2X4),
+                    scales=last_scales[b - 1][:],
+                    in_=last_grouped[b - 1][:].rearrange("p t j -> p (t j)"),
+                )
+                multiply(PASSES - 1, b - 1, last_codes[b - 1][:], last_scales[b - 1][:])
+                if b < BLOCKS:
+                    finish(nc.scalar.copy, b - 1, 0, D)
+        finish(nc.vector.tensor_copy, BLOCKS - 1, 0, D // 2)
+        finish(nc.vector.tensor_copy, BLOCKS - 1, D // 2, D)

@@ -22,12 +22,15 @@ W4_PASSES = 3
 BLOCKS = 4
 HALF = T // 2
 V_COLS = 320
+V_HALF = 160
+WHOLE = 3
+HALVES = ((3, 0), (4, 0), (3, 1), (4, 1))
 
 
 def load_scales(nc, plane, scales, passes):
     rows = scales.bitcast(I32).rearrange("a (q r) d -> r q a d", r=4)
     for r in range(4):
-        nc.gpsimd.dma_start(
+        nc.scalar.dma_start(
             out=plane[r:P:32, :].bitcast(I32).rearrange("q (a d) -> q a d", a=passes), in_=rows[r]
         )
 
@@ -48,14 +51,14 @@ def tile_mix_dyq_tm_none_kernel(tc, dy, w8_words, w8_scales, w4_words, w4_scales
         psum = ctx.enter_context(tc.psum_pool(name="psum", bufs=1))
         ctx.enter_context(tc.manual_schedule())
 
-        raw = [keep.tile([P, J, T], F32, name="raw%d" % g, align_bytes=64) for g in range(PASSES - 1)]
-        grouped = [keep.tile([P, T, J], BF16, name="grouped%d" % g, align_bytes=64) for g in range(PASSES - 1)]
-        codes = [keep.tile([P, T], U32, name="codes%d" % g, align_bytes=64) for g in range(PASSES - 1)]
-        scales = [keep.tile([P, T], U8, name="scales%d" % g, align_bytes=64) for g in range(PASSES - 1)]
-        last_raw = [keep.tile([P, J, P], F32, name="last_raw%d" % b, align_bytes=64) for b in range(BLOCKS)]
-        last_grouped = [keep.tile([P, P, J], BF16, name="last_grouped%d" % b, align_bytes=64) for b in range(BLOCKS)]
-        last_codes = [keep.tile([P, P], U32, name="last_codes%d" % b, align_bytes=64) for b in range(BLOCKS)]
-        last_scales = [keep.tile([P, P], U8, name="last_scales%d" % b, align_bytes=64) for b in range(BLOCKS)]
+        raw = [keep.tile([P, J, T], F32, name="raw%d" % g, align_bytes=64) for g in range(WHOLE)]
+        grouped = [keep.tile([P, T, J], BF16, name="grouped%d" % g, align_bytes=64) for g in range(WHOLE)]
+        codes = [keep.tile([P, T], U32, name="codes%d" % g, align_bytes=64) for g in range(WHOLE)]
+        scales = [keep.tile([P, T], U8, name="scales%d" % g, align_bytes=64) for g in range(WHOLE)]
+        half_raw = {u: keep.tile([P, J, HALF], F32, name="raw%d_%d" % u, align_bytes=64) for u in HALVES}
+        half_grouped = {u: keep.tile([P, HALF, J], BF16, name="grouped%d_%d" % u, align_bytes=64) for u in HALVES}
+        half_codes = {u: keep.tile([P, HALF], U32, name="codes%d_%d" % u, align_bytes=64) for u in HALVES}
+        half_scales = {u: keep.tile([P, HALF], U8, name="scales%d_%d" % u, align_bytes=64) for u in HALVES}
         w8 = keep.tile([P, W8_PASSES, D * 4], U8, name="w8", align_bytes=64)
         w4 = keep.tile([P, W4_PASSES, D * 2], U8, name="w4", align_bytes=64)
         w8_plane = keep.tile([P, W8_PASSES * D], U8, name="w8_plane", align_bytes=64)
@@ -65,6 +68,11 @@ def tile_mix_dyq_tm_none_kernel(tc, dy, w8_words, w8_scales, w4_words, w4_scales
         table_out = keep.tile([P, 1], F32, name="table_out")
         acc = [psum.tile([P, D], F32, name="acc%d" % b) for b in range(BLOCKS)]
 
+        nc.vector.memset(w8_plane[:].bitcast(I32), 0)
+        nc.vector.memset(w4_plane[:].bitcast(I32), 0)
+        nc.vector.memset(table_in[:], 0.0)
+
+        load_scales(nc, w8_plane, w8_scales, W8_PASSES)
         nc.sync.dma_start(out=raw[0][:], in_=dy_rows[0])
         nc.sync.dma_start(
             out=w8[:].rearrange("p a b -> p (a b)").bitcast(I32).rearrange("p (a b) -> p a b", a=W8_PASSES),
@@ -75,18 +83,11 @@ def tile_mix_dyq_tm_none_kernel(tc, dy, w8_words, w8_scales, w4_words, w4_scales
             out=w4[:].rearrange("p a b -> p (a b)").bitcast(I32).rearrange("p (a b) -> p a b", a=W4_PASSES),
             in_=w4_words.rearrange("a p b -> p a b").bitcast(I32),
         )
-        nc.sync.dma_start(out=raw[2][:], in_=dy_rows[2])
-        nc.sync.dma_start(out=raw[3][:], in_=dy_rows[3])
-        for b in range(BLOCKS):
-            nc.sync.dma_start(out=last_raw[b][:], in_=dy_rows[PASSES - 1][:, :, b * P : (b + 1) * P])
-
-        nc.vector.memset(w8_plane[:].bitcast(I32), 0)
-        nc.vector.memset(w4_plane[:].bitcast(I32), 0)
-        nc.vector.memset(table_in[:], 0.0)
-        load_scales(nc, w8_plane, w8_scales, W8_PASSES)
-        load_scales(nc, w4_plane, w4_scales, W4_PASSES)
-
         nc.scalar.copy(out=table_out[:], in_=table_in[:])
+        load_scales(nc, w4_plane, w4_scales, W4_PASSES)
+        nc.sync.dma_start(out=raw[2][:], in_=dy_rows[2])
+        for g, h in HALVES:
+            nc.sync.dma_start(out=half_raw[g, h][:], in_=dy_rows[g][:, :, h * HALF : (h + 1) * HALF])
 
         def multiply(g, b, b_codes, b_scales):
             if g < W8_PASSES:
@@ -106,7 +107,7 @@ def tile_mix_dyq_tm_none_kernel(tc, dy, w8_words, w8_scales, w4_words, w4_scales
                 stop=(g == PASSES - 1),
             )
 
-        for g in range(PASSES - 1):
+        for g in range(WHOLE):
             interleave(nc.scalar.copy, grouped[g], raw[g], V_COLS, T)
             interleave(nc.vector.tensor_copy, grouped[g], raw[g], 0, HALF)
             interleave(nc.vector.tensor_copy, grouped[g], raw[g], HALF, V_COLS)
@@ -124,17 +125,21 @@ def tile_mix_dyq_tm_none_kernel(tc, dy, w8_words, w8_scales, w4_words, w4_scales
             copy(out=result[b][:, d0:d1], in_=acc[b][:, d0:d1])
             nc.sync.dma_start(out=out[b * P : (b + 1) * P, d0:d1], in_=result[b][:, d0:d1])
 
-        for b in range(BLOCKS + 1):
-            if b < BLOCKS:
-                interleave(nc.vector.tensor_copy, last_grouped[b], last_raw[b], 0, P)
-            if b > 0:
+        for u in HALVES:
+            g, h = u
+            interleave(nc.scalar.copy, half_grouped[u], half_raw[u], V_HALF, HALF)
+            interleave(nc.vector.tensor_copy, half_grouped[u], half_raw[u], 0, V_HALF)
+            for b in (0, 1):
+                cols = slice(b * P, (b + 1) * P)
                 nc.vector.quantize_mx(
-                    out=last_codes[b - 1][:].bitcast(E5M2X4),
-                    scales=last_scales[b - 1][:],
-                    in_=last_grouped[b - 1][:].rearrange("p t j -> p (t j)"),
+                    out=half_codes[u][:, cols].bitcast(E5M2X4),
+                    scales=half_scales[u][:, cols],
+                    in_=half_grouped[u][:, cols, :].rearrange("p t j -> p (t j)"),
                 )
-                multiply(PASSES - 1, b - 1, last_codes[b - 1][:], last_scales[b - 1][:])
-                if b < BLOCKS:
-                    finish(nc.scalar.copy, b - 1, 0, D)
-        finish(nc.vector.tensor_copy, BLOCKS - 1, 0, D // 2)
-        finish(nc.vector.tensor_copy, BLOCKS - 1, D // 2, D)
+                multiply(g, 2 * h + b, half_codes[u][:, cols], half_scales[u][:, cols])
+            if u == (3, 1):
+                finish(nc.scalar.copy, 0, 0, D)
+        finish(nc.scalar.copy, 1, 0, D)
+        finish(nc.scalar.copy, 2, 0, D)
+        finish(nc.vector.tensor_copy, 3, 0, D // 2)
+        finish(nc.vector.tensor_copy, 3, D // 2, D)

from contextlib import ExitStack

import concourse.mybir as mybir

K, T, D = 2560, 512, 512
FLOPS = 2 * K * T * D

F32 = mybir.dt.float32
BF16 = mybir.dt.bfloat16
I32 = mybir.dt.int32
U32 = mybir.dt.uint32
U8 = mybir.dt.uint8
E5M2X4 = mybir.dt.float8_e5m2_x4
E4M3X4 = mybir.dt.float8_e4m3fn_x4
E2M1X4 = mybir.dt.float4_e2m1fn_x4

P = 128
J = 4
PASSES = 5
W8_PASSES = 2
W4_PASSES = 3
BLOCKS = 4
HALF = T // 2
V_COLS = 320
V_HALF = 160
WHOLE = 3
HALVES = ((3, 0), (4, 0), (3, 1), (4, 1))


def load_scales(nc, plane, scales, passes):
    rows = scales.bitcast(I32).rearrange("a (q r) d -> r q a d", r=4)
    for r in range(4):
        nc.scalar.dma_start(
            out=plane[r:P:32, :].bitcast(I32).rearrange("q (a d) -> q a d", a=passes), in_=rows[r]
        )


def interleave(copy, grouped, raw, t0, t1):
    copy(
        out=grouped[:, t0:t1, :].rearrange("p (c i) j -> p c j i", i=4),
        in_=raw[:, :, t0:t1].rearrange("p j (c i) -> p c j i", i=4),
    )


def tile_mix_dyq_tm_none_kernel(tc, dy, w8_words, w8_scales, w4_words, w4_scales, out):
    nc = tc.nc
    dy_rows = dy.rearrange("(g p j) t -> g p j t", p=P, j=J)

    with ExitStack() as ctx:
        keep = ctx.enter_context(tc.tile_pool(name="keep", bufs=1))
        psum = ctx.enter_context(tc.psum_pool(name="psum", bufs=1))
        ctx.enter_context(tc.manual_schedule())

        raw = [keep.tile([P, J, T], F32, name="raw%d" % g, align_bytes=64) for g in range(WHOLE)]
        grouped = [keep.tile([P, T, J], BF16, name="grouped%d" % g, align_bytes=64) for g in range(WHOLE)]
        codes = [keep.tile([P, T], U32, name="codes%d" % g, align_bytes=64) for g in range(WHOLE)]
        scales = [keep.tile([P, T], U8, name="scales%d" % g, align_bytes=64) for g in range(WHOLE)]
        half_raw = {u: keep.tile([P, J, HALF], F32, name="raw%d_%d" % u, align_bytes=64) for u in HALVES}
        half_grouped = {u: keep.tile([P, HALF, J], BF16, name="grouped%d_%d" % u, align_bytes=64) for u in HALVES}
        half_codes = {u: keep.tile([P, HALF], U32, name="codes%d_%d" % u, align_bytes=64) for u in HALVES}
        half_scales = {u: keep.tile([P, HALF], U8, name="scales%d_%d" % u, align_bytes=64) for u in HALVES}
        w8 = keep.tile([P, W8_PASSES, D * 4], U8, name="w8", align_bytes=64)
        w4 = keep.tile([P, W4_PASSES, D * 2], U8, name="w4", align_bytes=64)
        w8_plane = keep.tile([P, W8_PASSES * D], U8, name="w8_plane", align_bytes=64)
        w4_plane = keep.tile([P, W4_PASSES * D], U8, name="w4_plane", align_bytes=64)
        result = [keep.tile([P, D], F32, name="result%d" % b, align_bytes=64) for b in range(BLOCKS)]
        table_in = keep.tile([P, 1], F32, name="table_in")
        table_out = keep.tile([P, 1], F32, name="table_out")
        acc = [psum.tile([P, D], F32, name="acc%d" % b) for b in range(BLOCKS)]

        nc.vector.memset(w8_plane[:].bitcast(I32), 0)
        nc.vector.memset(w4_plane[:].bitcast(I32), 0)
        nc.vector.memset(table_in[:], 0.0)

        load_scales(nc, w8_plane, w8_scales, W8_PASSES)
        nc.sync.dma_start(out=raw[0][:], in_=dy_rows[0])
        nc.sync.dma_start(
            out=w8[:].rearrange("p a b -> p (a b)").bitcast(I32).rearrange("p (a b) -> p a b", a=W8_PASSES),
            in_=w8_words.rearrange("a p d i -> p a (d i)").bitcast(I32),
        )
        nc.sync.dma_start(out=raw[1][:], in_=dy_rows[1])
        nc.sync.dma_start(
            out=w4[:].rearrange("p a b -> p (a b)").bitcast(I32).rearrange("p (a b) -> p a b", a=W4_PASSES),
            in_=w4_words.rearrange("a p b -> p a b").bitcast(I32),
        )
        nc.scalar.copy(out=table_out[:], in_=table_in[:])
        load_scales(nc, w4_plane, w4_scales, W4_PASSES)
        nc.sync.dma_start(out=raw[2][:], in_=dy_rows[2])
        for g, h in HALVES:
            nc.sync.dma_start(out=half_raw[g, h][:], in_=dy_rows[g][:, :, h * HALF : (h + 1) * HALF])

        def multiply(g, b, b_codes, b_scales):
            if g < W8_PASSES:
                words = w8[:, g, :].bitcast(E4M3X4)
                plane = w8_plane[:, g * D : (g + 1) * D]
            else:
                a = g - W8_PASSES
                words = w4[:, a, :].bitcast(E2M1X4)
                plane = w4_plane[:, a * D : (a + 1) * D]
            nc.tensor.matmul_mx(
                out=acc[b][:],
                lhsT=b_codes.bitcast(E5M2X4),
                lhsT_scale=b_scales,
                rhs=words,
                rhs_scale=plane,
                start=(g == 0),
                stop=(g == PASSES - 1),
            )

        for g in range(WHOLE):
            interleave(nc.scalar.copy, grouped[g], raw[g], V_COLS, T)
            interleave(nc.vector.tensor_copy, grouped[g], raw[g], 0, HALF)
            interleave(nc.vector.tensor_copy, grouped[g], raw[g], HALF, V_COLS)
            for t0 in (0, HALF):
                nc.vector.quantize_mx(
                    out=codes[g][:, t0 : t0 + HALF].bitcast(E5M2X4),
                    scales=scales[g][:, t0 : t0 + HALF],
                    in_=grouped[g][:, t0 : t0 + HALF, :].rearrange("p t j -> p (t j)"),
                )
            for b in range(BLOCKS):
                cols = slice(b * P, (b + 1) * P)
                multiply(g, b, codes[g][:, cols], scales[g][:, cols])

        def finish(copy, b, d0, d1):
            copy(out=result[b][:, d0:d1], in_=acc[b][:, d0:d1])
            nc.sync.dma_start(out=out[b * P : (b + 1) * P, d0:d1], in_=result[b][:, d0:d1])

        for u in HALVES:
            g, h = u
            interleave(nc.scalar.copy, half_grouped[u], half_raw[u], V_HALF, HALF)
            interleave(nc.vector.tensor_copy, half_grouped[u], half_raw[u], 0, V_HALF)
            for b in (0, 1):
                cols = slice(b * P, (b + 1) * P)
                nc.vector.quantize_mx(
                    out=half_codes[u][:, cols].bitcast(E5M2X4),
                    scales=half_scales[u][:, cols],
                    in_=half_grouped[u][:, cols, :].rearrange("p t j -> p (t j)"),
                )
                multiply(g, 2 * h + b, half_codes[u][:, cols], half_scales[u][:, cols])
            if u == (3, 1):
                finish(nc.scalar.copy, 0, 0, D)
        finish(nc.scalar.copy, 1, 0, D)
        finish(nc.scalar.copy, 2, 0, D)
        finish(nc.vector.tensor_copy, 3, 0, D // 2)
        finish(nc.vector.tensor_copy, 3, D // 2, D)
